import numpy as np, ml_dtypes
CORES = [3,7,11,15,131,135,139,143]
N = 8
BF = ml_dtypes.bfloat16
def gentries(a):
    return np.ascontiguousarray(a.reshape(8, 16, -1).transpose(0, 2, 1)).reshape(8, -1)
def gtable(e):
    e = np.asarray(e); return np.ascontiguousarray(e.reshape(8, -1, 16).transpose(0, 2, 1)).reshape(128, -1).astype(np.int32)
W, K, RO, LG = 2048, 2, 3, 3
def turn(rng):
    o = np.argsort(rng.random((8, W)), axis=1); p = np.zeros((8, W), np.int64); h = W >> 1
    np.put_along_axis(p, o[:, :h], o[:, h:], 1); np.put_along_axis(p, o[:, h:], o[:, :h], 1)
    return p
def near(rng, p, noise):
    b = rng.integers(0, 256, (8, 16, W)); lo = np.minimum(np.arange(W)[None, :], p)
    b = np.take_along_axis(b, lo[:, None, :], 2)
    return np.clip(b[None] + rng.integers(-noise, noise + 1, (N, 8, 16, W)), 0, 255)
def pack(x, m):
    return {"fr": np.ascontiguousarray(x.reshape(N, 128, W)).astype(np.float32).astype(BF), "ptr": np.stack([gtable(a) for a in m])}
def setup_inputs(rng):
    p = turn(rng); x = near(rng, p, 6)
    x = np.where(rng.random((N, 8, 1, W)) < 0.25, rng.integers(0, 256, (N, 8, 16, W)), x)
    x = np.where(rng.random((8, 1, W)) < 0.06, rng.integers(0, 256, (8, 16, 1)), x)
    share = rng.choice(np.array([0.3, 0.5, 0.7]), (N, 8, 1))
    m = np.where(rng.random((N, 8, W)) < share, p[None], rng.integers(0, W, (N, 8, W)))
    return pack(x, m)
def setup_inputs_alike(rng):
    v = np.arange(W); h = (v + (W >> 1)) & (W - 1); x = near(rng, np.tile(h, (8, 1)), 5); m = np.zeros((N, 8, W), np.int64)
    for r in range(N):
        o = rng.permutation(8)
        for g in range(8):
            k = int(o[g])
            if k == 0:
                m[r, g] = 0; x[r ^ 1, g, :, 0] = 255; x[r ^ 1, g, :, 1] = 254
            elif k == 1: m[r, g] = W - 1
            elif k == 2: m[r, g] = v
            elif k == 3: m[r, g] = (v + 1) & (W - 1)
            elif k == 4: m[r, g] = W - 1 - v
            elif k == 5: m[r, g] = rng.choice(np.array([0, 3, W >> 1, W - 1]), W)
            else: m[r, g] = np.where(rng.random(W) < 0.7, h, rng.integers(0, W, W))
    return pack(x, m)
def setup_inputs_corners(rng):
    v = np.arange(W); L = W >> 5; low = np.arange(L); x = rng.integers(0, 256, (N, 8, 16, W)); m = np.zeros((N, 8, W), np.int64)
    role = np.zeros(N >> 1, np.int64); c0 = int(rng.integers(0, N >> 1)); role[c0 ^ 1] = 1; flip = int(rng.integers(0, 2))
    rest = [c for c in range(N >> 1) if c != c0 and c != c0 ^ 1]
    for i in range(len(rest)): role[rest[i]] = 2 + (i ^ flip)
    D = rng.integers(0, 32, 8); D[int(rng.integers(0, 8))] = 0; side = rng.integers(0, 2, 8); lone = int(rng.integers(0, 8))
    for c in range(N >> 1):
        k = int(role[c])
        for g in range(8):
            a = 2 * c + (int(side[g]) ^ int(k == 1)); b = a ^ 1
            if k == 2:
                m[a, g] = (v + g) & (W - 1); m[b, g] = (v + 1 + g) & (W - 1)
                x[a, g] = 255 * rng.integers(0, 2, (1, W))
                x[b, g] = np.where(rng.random((1, W)) < 0.5, 255 * rng.integers(0, 2, (1, W)), x[b, g])
                continue
            if k == 3 and g & 1 == 1:
                m[a, g] = 0; m[b, g] = W - 1 if g & 2 == 2 else v
                continue
            if k == 3: w = rng.permutation(W)
            else:
                kind = 1 if k == 1 and g == lone else int(rng.integers(0, 4))
                if kind == 0: lo = low
                elif kind == 1: lo = L - 1 - low
                elif kind == 2: lo = low ^ 1
                else: lo = np.argsort(rng.random((32, L)), axis=1)
                w = (((np.arange(32)[:, None] + int(D[g]) + 4 * int(k == 1)) & 31) * L + lo).reshape(-1)
            m[a, g] = w; m[b, g, w] = v
            x[b, g][:, w] = np.clip(x[a, g] + rng.integers(-7, 8, (16, W)), 0, 255)
            if k == 3: m[a, g] = np.where(rng.random(W) < 0.5, rng.integers(0, W, W), m[a, g])
            if k == 1 and g == lone:
                u = L * int(rng.integers(0, 32)) + int(rng.integers(2, L)); m[a, g, u] = int(w[u]) ^ 1
    return pack(x, m)
def setup_inputs_ends(rng):
    p = turn(rng); v = np.arange(W); lo = np.minimum(v[None, :], p)
    kind = rng.integers(0, 3, (8, 1, W)); b = 255 * np.where(kind == 2, rng.integers(0, 2, (8, 16, W)), kind)
    b = np.take_along_axis(b, lo[:, None, :], 2)
    x = np.where(rng.random((N, 8, 1, W)) < 0.25, 255 * rng.integers(0, 2, (N, 8, 16, W)), b[None])
    one = (rng.random((N, 8, 1, W)) < 0.25) & (np.arange(16)[:, None] == rng.integers(0, 16, (N, 8, 1, W)))
    x = np.where(one, np.abs(x - 1), x)
    u = rng.random((8, W)); hit = np.minimum(u, np.take_along_axis(u, p, 1)) < 0.15
    m = np.where(hit[None] & (rng.random((N, 8, W)) < 0.9), p[None], (W - 1) * rng.integers(0, 2, (N, 8, W)))
    for r in range(N):
        for g in range(8):
            s = (r ^ g) & 1
            if s == 1: m[r, g, 0] = W - 1; m[r, g, W - 1] = 0
            else: m[r, g, 0] = 0; m[r, g, W - 1] = W - 1
            m[r, g, W - 2] = W - 1
            for c in (0, 1, 2, 3, W - 2, W - 1): x[r, g, :, c] = 255 * s
            t = g >> 1
            if t > 0: x[r, g, int(rng.integers(0, 16)), (0, W - 1, 0, 1)[t]] = abs(255 * s - 1)
    return pack(x, m)
def setup_inputs_spread(rng):
    p = turn(rng); x = near(rng, p, 3); lo = np.minimum(np.arange(W)[None, :], p)
    sh = np.take_along_axis(rng.integers(0, 8, (8, W)), lo, 1)[None]
    sh = np.where(rng.random((N, 8, W)) < 0.3, rng.integers(0, 8, (N, 8, W)), sh)
    x = (x >> sh[:, :, None, :]) * (rng.random((N, 8, 1, W)) > 0.0625)
    w = np.minimum((W * rng.random((N, 8, W)) ** 4).astype(np.int64), W - 1)
    w = np.where(rng.random((N, 8, 1)) < 0.5, w, W - 1 - w)
    m = np.where(rng.random((N, 8, W)) < 0.4, p[None], w)
    return pack(x, m)
def setup_inputs_ties(rng):
    p = turn(rng); pal = rng.choice(np.array([0, 1, 100, 127, 128, 254, 255]), (8, 16, 4))
    pal[:, 0, 0] = 0; pal[:, 1, 0] = 200; pal[:, :, 1] = pal[:, :, 0]; pal[:, 0, 1] = 200; pal[:, 1, 1] = 0
    pal[:, 0:2, 2] = 128; pal[:, 0:2, 3] = 5
    ix = rng.integers(0, 4, (N, 8, W))
    x = np.take_along_axis(np.tile(pal[None], (N, 1, 1, 1)), ix[:, :, None, :], 3)
    x = np.where(rng.random((N, 8, 1, W)) < 0.125, rng.integers(0, 256, (N, 8, 16, W)), x)
    m = np.where(rng.random((N, 8, W)) < 0.5, p[None], rng.integers(0, W, (N, 8, W)))
    return pack(x, m)
def check_inputs(d):
    bad = []
    for k, lo, hi in (("fr", 0, 255), ("ptr", 0, W - 1)):
        a = np.asarray(d[k]).astype(np.float64)
        if not (np.min(a) >= lo and np.max(a) <= hi): bad.append("range of " + k)
        if not np.all(a == np.floor(a)): bad.append("whole numbers in " + k)
    return bad
def reference(fr, ptr):
    x = fr.astype(np.float32).astype(np.int32).reshape(N, 8, 16, W)
    m = np.stack([gentries(a) for a in ptr]).astype(np.int64)
    cnt = [0] * N; own = np.arange(W)[None, :]
    for t in range(RO):
        h = 1 << (t % LG); chosen = []
        for r in range(N):
            a, n, xq = m[r], m[r ^ h], x[r ^ h]
            es = [a]
            for i in range(K): es.append(np.take_along_axis(a, np.take_along_axis(n, es[-1], 1), 1))
            es.append((np.roll(a, 1, axis=1) + 1 + (cnt[r] & 3)) & (W - 1))
            far = np.stack([np.sum(np.abs(np.take_along_axis(xq, e[:, None, :], 2) - x[r]), axis=1) for e in es])
            first = np.argmin(far, axis=0)
            chosen.append(np.take_along_axis(np.stack(es), first[None], 0)[0])
        lifted = []
        for r in range(N):
            q = r ^ h
            con = np.take_along_axis(chosen[q], chosen[r], 1) == own
            c = con[:, None, :]; y = np.take_along_axis(x[q], chosen[r][:, None, :], 2)
            if r < q: lifted.append(np.where(c, (x[r] + y) >> 1, x[r]))
            else:
                z = np.abs(x[r] - y); lifted.append(np.where(c, z, z >> 1))
            cnt[r] = int(np.sum(con))
        x = np.stack(lifted); m = np.stack(chosen)
    return {"yf": x.reshape(N, 128, W).astype(np.float32).astype(BF), "yp": np.stack([gtable(a) for a in m]).astype(np.float32)}

from concourse.bass import DstId, RemoteDMATransfer
from concourse.mybir import AluOpType, ActivationFunctionType

W = 2048
L = W // 16
RO = 3
BIG = float(1 << 24)
STEP1 = 1.5 * (1 << 23)
HALF = 1023.0 / 2048.0

SCRATCH = {
    "xb0": ("sbuf", [128, 2 * W], "bfloat16"), "xb1": ("sbuf", [128, 2 * W], "bfloat16"),
    "aw": ("sbuf", [128, 4 * W], "bfloat16"),
    "mrow": ("sbuf", [128, W], "bfloat16"), "nrow": ("sbuf", [128, W], "float32"), "prow": ("sbuf", [128, W], "bfloat16"),
    "ra": ("sbuf", [128, W], "bfloat16"), "rb": ("sbuf", [128, W], "bfloat16"), "rc": ("sbuf", [128, W], "bfloat16"),
    "hs": ("sbuf", [128, W], "float16"), "vrow": ("sbuf", [128, W], "float32"),
    "spread": ("sbuf", [128, W + 16], "bfloat16"), "z": ("sbuf", [128, 3, 144], "bfloat16"),
    "id1": ("sbuf", [128, 128], "bfloat16"), "id128": ("sbuf", [128, 128], "bfloat16"),
    "idm": ("sbuf", [128, 128], "bfloat16"), "idh": ("sbuf", [128, 128], "float16"),
    "ones": ("sbuf", [128, 128], "float32"),
    "idf": ("sbuf", [128, 128], "float32"), "shf": ("sbuf", [128, 128], "float32"), "wrp": ("sbuf", [128, 128], "float32"),
    "i3": ("sbuf", [128, 128], "int32"), "i2": ("sbuf", [128, 128], "int32"), "i4": ("sbuf", [128, 128], "int32"),
    "t8": ("sbuf", [128, 8], "int32"), "t8a": ("sbuf", [128, 8], "float32"), "t8b": ("sbuf", [128, 8], "float32"),
    "kmi": ("sbuf", [128, 8], "int32"), "kmf": ("sbuf", [128, 8], "float32"), "vf": ("sbuf", [128, L], "float32"),
    "key": ("sbuf", [128, L], "int32"), "best": ("sbuf", [128, L], "float32"), "mi": ("sbuf", [128, L], "int32"),
    "abi": ("sbuf", [128, 2, L], "int32"), "ab": ("sbuf", [128, 2, L], "bfloat16"), "ia": ("sbuf", [128, L], "uint16"),
    "ti": ("sbuf", [128, L], "int32"), "tj": ("sbuf", [128, L], "int32"), "tf": ("sbuf", [128, L], "float32"),
    "base0": ("sbuf", [128, L], "float32"), "base1": ("sbuf", [128, L], "float32"),
    "base2": ("sbuf", [128, L], "float32"), "base3": ("sbuf", [128, L], "float32"),
    "e0": ("sbuf", [128, L], "uint16"), "e1": ("sbuf", [128, L], "uint16"), "e2": ("sbuf", [128, L], "uint16"),
    "e3": ("sbuf", [128, L], "uint16"), "isel": ("sbuf", [128, L], "uint16"),
    "cf": ("sbuf", [128, 8], "float32"), "ci": ("sbuf", [128, 8], "int32"), "cj": ("sbuf", [128, 8], "int32"),
    "c1": ("sbuf", [128, 8], "float32"),
}
for _t in range(RO + 1):
    SCRATCH["ms%d" % _t] = ("sbuf", [128, L], "uint16")
for _t in range(RO):
    SCRATCH["xp%d" % _t] = ("sbuf", [128, W], "bfloat16")
    SCRATCH["mf%d" % _t] = ("sbuf", [128, L], "float16")
    SCRATCH["min%d" % _t] = ("sbuf", [128, L], "float16")
    SCRATCH["snin%d" % _t] = ("sbuf", [128, L], "uint16")
for _t in range(4):
    SCRATCH["pr%d" % _t] = ("psum", [128, 512], "float32")
    SCRATCH["pq%d" % _t] = ("psum", [128, 512], "float32")

SEMAPHORES = ["qv", "qa", "qt", "qg", "ldp", "lda", "ldb", "sto", "sent"]
for _t in range(RO):
    SEMAPHORES += ["inx%d" % _t, "inm%d" % _t, "insn%d" % _t, "outx%d" % _t]


def rank_program(g, core, T, topo):
    rank = T.rank_of(core)
    if rank is None:
        return
    A, F = AluOpType, ActivationFunctionType
    V, S, P = g.vector, g.scalar, g.tensor
    Q = {"v": V, "a": S, "t": P, "g": g, "s": g.sync}
    cnt = {}
    seen = {}
    log = {}
    H, R = W // 2, W // 4
    TAIL = W - W // 8
    FAR = 2048
    E0 = 320

    def wait(q, ev):
        s, n = ev
        if seen.get((q, s), 0) < n:
            Q[q].wait_ge(T.sem[s], n)
            seen[(q, s)] = n

    def span(r):
        return (r, 0, 1 << 20) if isinstance(r, str) else r

    def order(q, reads, writes):
        for w, rs in ((False, reads), (True, writes)):
            for r in rs:
                b, lo, hi = span(r)
                ps = SCRATCH[b][0] == "psum"
                for (l2, h2, w2, ev, q2) in log.get(b, []):
                    if l2 < hi and lo < h2 and (w or w2 or (ps and q2 != q)) and not (q == "t" and q2 == "t"):
                        wait(q, ev)

    def note(q, reads, writes, ev):
        for w, rs in ((False, reads), (True, writes)):
            for r in rs:
                b, lo, hi = span(r)
                log.setdefault(b, []).append((lo, hi, w, ev, q))

    def bump(s, n):
        cnt[s] = cnt.get(s, 0) + n
        return (s, cnt[s])

    def op(q, fn, reads, writes):
        order(q, reads, writes)
        fn().then_inc(T.sem["q" + q], 1)
        note(q, reads, writes, bump("q" + q, 1))

    def dma(q, sem, out, in_, reads, writes):
        order(q, reads, writes)
        Q[q].dma_start(out, in_).then_inc(T.sem[sem], 16)
        note("d", reads, writes, bump(sem, 16))

    def bits(engs):
        return sum(1 << e for e in engs)

    def send(dst, parts, rsem, lsem):
        rid, pid = topo.addr(dst, core)
        order("g", [p[3] for p in parts], [])
        if len(parts) == 1:
            s, d, e, _ = parts[0]
            g.remote_dma(d, s, T.sem[rsem], T.sem[lsem], pid, rid, bits(e))
        else:
            g.remote_dma_fused([RemoteDMATransfer(dst_ids=[DstId(rid=rid, pnc=pid)], dma_engine_mask=bits(e),
                                                  remote_sem=T.sem[rsem], src=s, dst=d) for s, d, e, _ in parts],
                               local_sem=T.sem[lsem])
        return sum(len(p[2]) for p in parts)

    def lands(buf, sem, n):
        note("d", [], [buf], bump(sem, n))

    def ts(out, in0, s1, s2, o0, o1, reads, writes):
        if o1 is None:
            op("v", lambda: V.tensor_scalar(out, in0, s1, None, o0), reads, writes)
        else:
            op("v", lambda: V.tensor_scalar(out, in0, s1, s2, o0, o1), reads, writes)

    def tt(out, in0, in1, o, reads, writes):
        op("v", lambda: V.tensor_tensor(out, in0, in1, o), reads, writes)

    def fill(ap, x, writes):
        op("v", lambda: V.memset(ap, x), [], writes)

    def act(out, in_, f, reads, writes, **k):
        op("a", lambda: S.activation(out, in_, f, **k), reads, writes)

    def cp(q, out, in_, reads, writes):
        if q == "v":
            op("v", lambda: V.tensor_copy(out, in_), reads, writes)
        else:
            act(out, in_, F.Copy, reads, writes)

    def mm(items, reads, writes):
        def fn():
            last = None
            for it in items:
                last = P.matmul(*it)
            return last
        op("t", fn, reads, writes)

    def gather(q, out, o0, win, wn, lst, l0, a, b):
        cp(q, T[out][:, o0 + a:o0 + b], T[win][:, 0:wn].indirect(T[lst][:, l0 + a // 16:l0 + b // 16]),
           [(win, 0, wn), (lst, l0 + a // 16, l0 + b // 16)], [(out, o0 + a, o0 + b)])

    def to_list(bank, m, row, r0, a, b, start, stop):
        mm([(T[bank][:, a // 16:b // 16], T.z[:, m, 15 - i:143 - i], T[row][:, r0 + a + i:r0 + b:16],
             start and i == 0, stop and i == 15) for i in range(16)], ["z", (row, r0 + a, r0 + b)], [bank])

    def to_window(srcs, reads, row, engs):
        for j in range(4):
            bk = "pr%d" % j
            mm([(T[bk][:, 128 * (i % 4):128 * (i % 4) + 128], T.spread[:, 1 - n + 128 * i:129 - n + 128 * i], s,
                 n == 0, n == len(srcs) - 1) for i in range(4 * j, 4 * j + 4) for n, s in enumerate(srcs)],
               ["spread"] + reads, [bk])
            cp(engs[j], T[row][:, R * j:R * j + R], T[bk][:, :], [bk], [(row, R * j, R * j + R)])

    def parts(a, b):
        ts(T.abi[:, 0, a:b], T.key[:, a:b], 4, 127, A.arith_shift_right, A.bitwise_and, [("key", a, b)], [("abi", a, b)])
        ts(T.abi[:, 1, a:b], T.key[:, a:b], 15, None, A.bitwise_and, None, [("key", a, b)], [("abi", L + a, L + b)])
        cp("v", T.ab[:, :, a:b], T.abi[:, :, a:b], [("abi", a, b), ("abi", L + a, L + b)], [("ab", a, b)])
        if b == L:
            mm([(T.pq0[:, 0:L], T.id1[:, :], T.ab[:, 0, :], True, False),
                (T.pq0[:, 0:L], T.id128[:, :], T.ab[:, 1, :], False, True)], ["id1", "id128", "ab"], ["pq0"])

    def shift():
        mm([(T.pq2[:, 0:L], T.shf[:, :], T.base0[:, :], True, False),
            (T.pq2[:, 1:L], T.wrp[:, :], T.base0[:, 0:L - 1], False, False),
            (T.pq2[:, 0:1], T.wrp[:, :], T.base0[:, L - 1:L], False, True)], ["shf", "wrp", "base0"], ["pq2"])

    def last_candidate(t):
        c = 1.0 if t == 0 else T.c1[:, 0:1]
        ts(T.ti[:, :], T.pq2[:, 0:L], BIG, c, A.add, A.add, ["pq2", "c1"], ["ti"])
        ts(T.tj[:, :], T.ti[:, :], W - 1, None, A.bitwise_and, None, ["ti"], ["tj"])
        cp("v", T.e3[:, :], T.tj[:, :], ["tj"], ["e3"])
        ts(T.base3[:, :], T.tj[:, :], 3.0 * W - BIG, None, A.add, None, ["tj"], ["base3"])

    def link(k, bank):
        cp("v", T["e%d" % k][:, :], T[bank][:, 0:L], [bank], ["e%d" % k])
        ts(T["base%d" % k][:, :], T[bank][:, 0:L], k * W - BIG, None, A.add, None, [bank], ["base%d" % k])

    mate = [T.cores[rank ^ (1 << t)] for t in range(RO)]
    eng = [topo.engines(core, c) for c in mate]
    back = [len(topo.engines(c, core)) for c in mate]

    dma("s", "ldp", T.key[:, :], T.ptr[:, :], [], ["key"])
    dma("a", "lda", T.xb0[:, 0:H], T.fr[:, 0:H], [], [("xb0", 0, H)])
    dma("s", "ldb", T.xb0[:, H:W], T.fr[:, H:W], [], [("xb0", H, W)])
    op("g", lambda: g.iota(T.i3[:, :], [[-1, 128]], 0, 1), [], ["i3"])
    op("g", lambda: g.iota(T.i2[:, :], [[-1, 16], [-16, 8]], 0, 1), [], ["i2"])
    op("g", lambda: g.iota(T.i4[:, :], [[16, 128]], 0, 0), [], ["i4"])
    fill(T.spread[:, :], 0.0, ["spread"])
    ts(T.id1[:, :], T.i3[:, :], 0.0, None, A.is_equal, None, ["i3"], ["id1"])
    act(T.id128[:, :], T.id1[:, :], F.Copy, ["id1"], ["id128"], scale=128.0)
    act(T.idf[:, :], T.id1[:, :], F.Copy, ["id1"], ["idf"])
    act(T.idm[:, :], T.id1[:, :], F.Copy, ["id1"], ["idm"], scale=-1.0)
    ts(T.spread[:, 1:W + 1:16], T.i2[:, :], 0.0, None, A.is_equal, None, ["i2"], ["spread"])
    fill(T.z[:, :, :], 0.0, ["z"])
    fill(T.wrp[:, :], 0.0, ["wrp"])
    fill(T.ones[:, :], 1.0, ["ones"])
    parts(0, L)
    e0, half = eng[0], len(eng[0]) // 2
    n = send(mate[0], [(T.xb0[:, 0:H], T.xp0[:, 0:H], e0[half:], ("xb0", 0, H))], "inx0", "outx0")
    cp("v", T.e0[:, :], T.key[:, :], ["key"], ["e0"])
    cp("v", T.ms0[:, 0:L], T.pq0[:, 0:L], ["pq0"], ["ms0"])
    bump("sent", send(mate[0], [(T.ms0[:, 0:L], T.snin0[:, :], e0[:half], "ms0")], "insn0", "sent"))
    n += send(mate[0], [(T.xb0[:, H:W], T.xp0[:, H:W], e0[:half], ("xb0", H, W))], "inx0", "outx0")
    note("d", [("xb0", 0, W)], [], bump("outx0", n))
    lands("xp0", "inx0", back[0])
    lands("snin0", "insn0", back[0] // 2)
    op("g", lambda: g.iota(T.vrow[:, :], [[1, W]], 0, 0, allow_small_or_imprecise_dtypes=True), [], ["vrow"])
    to_window([T.ab[:, 0, :], T.ab[:, 1, :]], ["ab"], "mrow", "aaaa")
    ts(T.base0[:, :], T.key[:, :], -BIG, None, A.add, None, ["key"], ["base0"])
    ts(T.shf[:, :], T.i3[:, :], -1.0, None, A.is_equal, None, ["i3"], ["shf"])
    ts(T.wrp[:, 0:128:16], T.i3[:, 0:128:16], 15.0, None, A.is_equal, None, ["i3"], ["wrp"])
    fill(T.shf[:, 0:128:16], 0.0, ["shf"])
    shift()
    ts(T.t8[:, :], T.i3[:, 0:128:16], 4, None, A.arith_shift_right, None, ["i3"], ["t8"])
    ts(T.t8a[:, :], T.i3[:, 0:128:16], 0.0, 16.0, A.is_equal, A.mult, ["i3"], ["t8a"])
    ts(T.t8b[:, :], T.i3[:, 0:128:16], 1.0, None, A.is_equal, None, ["i3"], ["t8b"])
    ts(T.kmi[:, 0:1], T.i3[:, 0:1], 15, None, A.bitwise_and, None, ["i3"], ["kmi"])
    ts(T.z[:, 0, 15:143:16], T.t8[:, :], 0.0, 4.0 * W, A.is_equal, A.mult, ["t8"], [("z", 0, 1)])
    tt(T.z[:, 1, 15:143:16], T.t8a[:, :], T.t8b[:, :], A.add, ["t8a", "t8b"], [("z", 1, 2)])
    ts(T.z[:, 2, 15:143:16], T.t8a[:, :], W / 16.0, None, A.mult, None, ["t8a"], [("z", 2, 3)])
    cp("v", T.kmf[:, 0:1], T.kmi[:, 0:1], ["kmi"], ["kmf"])
    ts(T.idh[:, :], T.id1[:, :], HALF, None, A.mult, None, ["id1"], ["idh"])
    last_candidate(0)
    ts(T.vf[:, :], T.i4[:, :], T.kmf[:, 0:1], None, A.add, None, ["i4", "kmf"], ["vf"])
    gather("v", "prow", 0, "mrow", W, "snin0", 0, 0, H)
    gather("a", "prow", 0, "mrow", W, "snin0", 0, H, W)

    for t in range(RO):
        low = rank < rank ^ (1 << t)
        last = t == RO - 1
        xb, xn, xp, mn = "xb%d" % (t % 2), "xb%d" % (1 - t % 2), "xp%d" % t, "ms%d" % (t + 1)
        bank = {0: ("pr0", "pr0"), 3: ("pr1", "pr1"), 1: ("pr2", "pq0"), 2: ("pr3", "pq1")}

        def diff(k, a, b):
            e = "e%d" % k
            tt(T.aw[:, k * W + a:k * W + b], T[xp][:, :].indirect(T[e][:, a // 16:b // 16]), T[xb][:, a:b], A.subtract,
               [xp, (e, a // 16, b // 16), (xb, a, b)], [("aw", k * W + a, k * W + b)])

        def mag(k, a, b):
            r = ("aw", k * W + a, k * W + b)
            act(T.aw[:, r[1]:r[2]], T.aw[:, r[1]:r[2]], F.Abs, [r], [r])

        def keys(k, a, b):
            bk = bank[k][a >= H]
            lo, hi = (0, L) if k in (0, 3) else (L // 2, L) if a >= H else (0, L // 2)
            if a == 16 * lo:
                mm([(T[bk][:, lo:hi], T.idf[:, :], T["base%d" % k][:, lo:hi], True, False)], ["idf", "base%d" % k], [bk])
            to_list(bk, 0, "aw", k * W, a, b, False, b == 16 * hi)

        def dist(k, a, b):
            mag(k, a, b)
            keys(k, a, b)

        def far_sub(j):
            a, b, bk = j * R, min(j * R + R, FAR), "pq%d" % (2 + j % 2)
            if a < b:
                mm([(T[bk][:, 0:b - a], T.id1[:, :], T.rc[:, a:b], True, False),
                    (T[bk][:, 0:b - a], T.idm[:, :], T[xb][:, a:b], False, True)], ["id1", "idm", ("rc", a, b), (xb, a, b)], [bk])

        def far_abs(j):
            a, b, bk = j * R, min(j * R + R, FAR), "pq%d" % (2 + j % 2)
            if a < b:
                act(T.aw[:, 3 * W + a:3 * W + b], T[bk][:, 0:b - a], F.Abs, [bk], [("aw", 3 * W + a, 3 * W + b)])

        def least(k, a=0, b=L):
            bk = bank[k][a > 0]
            if k == 0:
                cp("v", T.best[:, :], T[bk][:, 0:L], [bk], ["best"])
            else:
                o = "key" if k == 2 else "best"
                tt(T[o][:, a:b], T[bk][:, a:b], T.best[:, a:b], A.min, [bk, "best"], [(o, a, b)])

        if t == 0:
            gather("v", "rb", 0, "prow", W, "e0", 0, 0, H)
            gather("a", "rb", 0, "prow", W, "e0", 0, H, W)
            to_list("pq0", 1, "rb", 0, 0, W, True, True)
            diff(0, 0, H)
            gather("a", "rc", 0, xp, W, "e3", 0, 0, H)
        else:
            gather("v", "rb", 0, "prow", W, "e0", 0, E0, H)
            to_list("pr2", 1, "rb", 0, 0, H, True, True)
            gather("a", "rb", 0, "prow", W, "e0", 0, H, W)
            to_list("pr2", 1, "rb", 0, H, W, True, True)
            cp("v", T.ci[:, 0:1], T.pq3[:, 0:1], ["pq3"], ["ci"])
            ts(T.cj[:, 0:1], T.ci[:, 0:1], 3, None, A.bitwise_and, None, ["ci"], ["cj"])
            ts(T.c1[:, 0:1], T.cj[:, 0:1], 1.0, None, A.add, None, ["cj"], ["c1"])
            last_candidate(t)
        link(1, "pr2" if t else "pq0")
        gather("v", "ra", 0, "prow", W, "e1", 0, 0, H)
        gather("a", "ra", 0, "prow", W, "e1", 0, H, W)
        to_list("pq1", 1, "ra", 0, 0, W, True, True)
        if t > 0:
            diff(0, 0, H)
            gather("a", "rc", 0, xp, W, "e3", 0, 0, H)
            link(2, "pq1")
        gather("a", "rc", 0, xp, W, "e3", 0, H, FAR)
        diff(0, H, W)
        if t == 0:
            link(2, "pq1")
        far_sub(0)
        far_sub(1)
        dist(0, 0, H)
        far_abs(0)
        far_abs(1)
        far_sub(2)
        far_sub(3)
        if FAR < W:
            diff(3, FAR, W)
        keys(3, 0, H)
        diff(1, 0, H)
        dist(0, H, W)
        far_abs(2)
        far_abs(3)
        if FAR < W:
            mag(3, FAR, W)
        keys(3, H, W)
        diff(2, 0, H)
        dist(1, 0, H)
        diff(1, H, W)
        dist(2, 0, H)
        least(0)
        diff(2, H, TAIL)
        diff(2, TAIL, W)
        dist(1, H, W)
        mag(2, H, TAIL)
        mag(2, TAIL, W)
        keys(2, H, W)
        least(3)
        mf = "mf%d" % t
        least(1, 0, L // 2)
        for a, b in ((0, L // 2), (L // 2, L)):
            least(2, a, b)
            ts(T.mi[:, a:b], T.key[:, a:b], W - 1, None, A.bitwise_and, None, [("key", a, b)], [("mi", a, b)])
            if not low:
                ts(T.ti[:, a:b], T.key[:, a:b], 3 * W, None, A.bitwise_and, None, [("key", a, b)], [("ti", a, b)])
            cp("v", T[mf][:, a:b], T.mi[:, a:b], [("mi", a, b)], [(mf, a, b)])
            if b == L:
                bump("sent", send(mate[t], [(T[mf][:, :], T["min%d" % t][:, :], eng[t], mf)], "inm%d" % t, "sent"))
                lands("min%d" % t, "inm%d" % t, back[t])
            parts(a, b)
            if low:
                cp("v", T.e0[:, a:b], T.mi[:, a:b], [("mi", a, b)], [("e0", a, b)])
            else:
                tt(T.tf[:, a:b], T.ti[:, a:b], T.vf[:, a:b], A.add, [("ti", a, b), "vf"], [("tf", a, b)])
                cp("v", T.ia[:, a:b], T.tf[:, a:b], [("tf", a, b)], [("ia", a, b)])
            if a == 0:
                least(1, b, L)
                if low:
                    gather("a", "rc", 0, xp, W, "e0", 0, 0, H)
                else:
                    gather("a", xb, W, "aw", 4 * W, "ia", 0, 0, H)
        cp("v", T[mn][:, 0:L], T.pq0[:, 0:L], ["pq0"], [mn])
        if not last:
            bump("sent", send(mate[t + 1], [(T[mn][:, 0:L], T["snin%d" % (t + 1)][:, :], eng[t + 1], mn)],
                              "insn%d" % (t + 1), "sent"))
            lands("snin%d" % (t + 1), "insn%d" % (t + 1), back[t + 1])
            to_window([T.ab[:, 0, :], T.ab[:, 1, :]], ["ab"], "mrow", "aaaa")
        if low:
            tt(T.hs[:, H:W], T[xp][:, :].indirect(T.e0[:, L // 2:L]), T[xb][:, H:W], A.add, [xp, "e0", (xb, H, W)], [("hs", H, W)])
            ts(T.hs[:, H:W], T.hs[:, H:W], 0.5, 1023.75, A.mult, A.add, [("hs", H, W)], [("hs", H, W)])
            for a in (0, R):
                bk = "pq%d" % (2 + a // R)
                mm([(T[bk][:, :], T.idh[:, :], T.rc[:, a:a + R], True, False),
                    (T[bk][:, :], T.idh[:, :], T[xb][:, a:a + R], False, True)], ["idh", ("rc", a, a + R), (xb, a, a + R)], [bk])
                ts(T[xb][:, W + a:W + a + R], T[bk][:, :], STEP1, STEP1, A.add, A.subtract, [bk], [(xb, W + a, W + a + R)])
        else:
            gather("v", xb, W, "aw", 4 * W, "ia", 0, H, W)
            ts(T.hs[:, :], T[xb][:, W:2 * W], 0.5, 1023.75, A.mult, A.add, [(xb, W, 2 * W)], ["hs"])
        o = W if low else 0
        if not low:
            ts(T[xb][:, o:o + H], T.hs[:, 0:H], -1024.0, None, A.add, None, ["hs"], [(xb, o, o + H)])
        if last:
            cp("v", T.base0[:, :], T.mi[:, :], ["mi"], ["base0"])
            dma("s", "sto", T.yp[:, :], T.base0[:, :], ["base0"], [])

        to_window([T["min%d" % t][:, :]], ["min%d" % t], "nrow", "aaav" if last else "avav")
        for bk, a in (("pq1", 0), ("pq0", L // 2)):
            mm([(T[bk][:, a:a + L // 2], T.idf[:, :], T.vf[:, a:a + L // 2], True, False)], ["idf", "vf"], [bk])
        if not last:
            gather("a", "prow", 0, "mrow", W, "snin%d" % (t + 1), 0, 0, W)

        def claim(bk, a, b):
            tt(T.ra[:, a:b], T.nrow[:, :].indirect(T[mn][:, a // 16:b // 16]), T.vrow[:, a:b], A.is_equal,
               ["nrow", mn, "vrow"], [("ra", a, b)])
            to_list(bk, 2, "ra", 0, a, b, False, True)

        claim("pq1", 0, H)
        ts(T[xb][:, o + H:o + W], T.hs[:, H:W], -1024.0, None, A.add, None, ["hs"], [(xb, o + H, o + W)])
        if not low and not last:
            cp("v", T.e0[:, :], T.mi[:, :], ["mi"], ["e0"])
        cp("v", T.isel[:, 0:L // 2], T.pq1[:, 0:L // 2], ["pq1"], [("isel", 0, L // 2)])
        claim("pq0", H, W)
        if not last:
            ts(T.base0[:, :], T.mi[:, :], -BIG, None, A.add, None, ["mi"], ["base0"])
            shift()

        tot = 0
        for js in ((0,), (1,), (2, 3)):
            pieces = []
            for i, j in enumerate(js):
                a = j * R
                if j == 2:
                    if not last:
                        gather("a", "rb", 0, "prow", W, "e0", 0, 0, E0)
                    cp("v", T.isel[:, L // 2:L], T.pq0[:, L // 2:L], ["pq0"], [("isel", L // 2, L)])
                gather("v" if j == 2 else "a", xn, 0, xb, 2 * W, "isel", 0, a, a + R)
                if last:
                    dma("s", "sto", T.yf[:, a:a + R], T[xn][:, a:a + R], [(xn, a, a + R)], [])
                else:
                    m = len(eng[t + 1]) // len(js)
                    pieces.append((T[xn][:, a:a + R], T["xp%d" % (t + 1)][:, a:a + R], eng[t + 1][i * m:i * m + m], (xn, a, a + R)))
            if not last:
                tot += send(mate[t + 1], pieces, "inx%d" % (t + 1), "outx%d" % (t + 1))
        if not last:
            note("d", [(xn, 0, W)], [], bump("outx%d" % (t + 1), tot))
            lands("xp%d" % (t + 1), "inx%d" % (t + 1), 3 * back[t + 1])
            for i, bk in enumerate(("pq1", "pq0")):
                a = i * L // 2
                act(T.tf[:, a:a + L // 2], T[bk][:, a:a + L // 2], F.Copy, [bk], [("tf", a, a + L // 2), ("cf", 4 * i, 4 * i + 1)],
                    scale=1.0 / W, accum_out=T.cf[:, 4 * i:4 * i + 1])
            mm([(T.pq3[:, 0:1], T.ones[:, :], T.cf[:, 4 * i:4 * i + 1], i == 0, i == 1) for i in range(2)], ["ones", "cf"], ["pq3"])

    for s in sorted(cnt):
        wait("s" if s in ("sto", "ldp", "ldb") else "g", (s, cnt[s]))
